import numpy as np
import ml_dtypes


def mxq(x, axis, fmt="e4m3"):
    dtype, down = {"e4m3": (ml_dtypes.float8_e4m3fn, 7), "e5m2": (ml_dtypes.float8_e5m2, 14)}[fmt]
    v = np.moveaxis(np.asarray(x, np.float32).astype(ml_dtypes.bfloat16).astype(np.float64), axis, -1)
    blocks = v.reshape(v.shape[:-1] + (-1, 32))
    amax = np.abs(blocks).max(-1, keepdims=True)
    byte = np.maximum(np.where(amax > 0, np.frexp(amax)[1] - 1 + 127, 0) - down, 1)
    scale = np.exp2(byte - 127.0)
    codes = (blocks / scale).astype(np.float32).astype(dtype).astype(np.float64)
    return np.moveaxis((codes * scale).reshape(v.shape), -1, axis)


WIDE = False


def mx_kscale(k):
    if not WIDE:
        return np.ones(k)
    levels = np.array([10, -10, 5, -5, 0])
    if k % 512:
        return np.exp2(np.random.permutation(np.resize(levels, k // 32))).repeat(32)
    a = np.empty((k // 512, 16))
    for p in range(k // 512):
        a[p, :8] = np.random.permutation(np.resize(levels, 8))
        for g in range(8):
            far = levels[np.abs(levels - a[p, g]) >= 10]
            a[p, g + 8] = far[np.random.randint(len(far))]
    return np.exp2(a.ravel()).repeat(32)


def f64(x):
    return np.asarray(x).astype(np.float64)


def striped(idx):
    return np.tile(idx.reshape(-1, 16).T, (8, 1)).astype(np.uint16)


def unstriped(offs):
    return offs[:16].T.reshape(-1).astype(np.int64)


E2M1 = np.array([0.0, 0.5, 1.0, 1.5, 2.0, 3.0, 4.0, 6.0, -0.0, -0.5, -1.0, -1.5, -2.0, -3.0, -4.0, -6.0])


def pack_weight(w, fmt):
    k, n = w.shape
    w = f64(np.asarray(w, np.float32).astype(ml_dtypes.bfloat16)).reshape(k // 32, 32, n)
    amax = np.abs(w).max(1)
    if fmt == "e4m3":
        byte = np.frexp(amax)[1] - 1 + 127 - 7
    else:
        mant, ex = np.frexp(amax / 6.0)
        byte = np.where(mant > 0.5, ex, ex - 1) + 127
    byte = np.clip(np.where(amax > 0, byte, 1), 1, 254)
    scaled = (w * np.exp2(127.0 - byte)[:, None, :]).reshape(k, n).astype(np.float32)
    by_word = np.ascontiguousarray(scaled.reshape(k // 512, 128, 4, n).transpose(0, 1, 3, 2))
    if fmt == "e4m3":
        words = by_word.astype(ml_dtypes.float8_e4m3fn).view(np.uint8)
    else:
        c = by_word.astype(ml_dtypes.float4_e2m1fn).view(np.uint8) & 0xF
        words = (c[..., 0::2] | (c[..., 1::2] << 4)).reshape(k // 512, 128, 2 * n)
    return np.ascontiguousarray(words), np.ascontiguousarray(byte.astype(np.uint8).reshape(k // 512, 16, n))


def unpack_weight(words, scales, fmt):
    g, _, n = scales.shape
    words = np.ascontiguousarray(words).reshape(g, 128, n, -1)
    if fmt == "e4m3":
        vals = words.view(ml_dtypes.float8_e4m3fn).astype(np.float64)
    else:
        nib = np.empty((g, 128, n, 4), np.uint8)
        nib[..., 0::2] = words & 0xF
        nib[..., 1::2] = words >> 4
        vals = E2M1[nib]
    vals = vals * np.repeat(np.exp2(scales.astype(np.float64) - 127.0), 8, axis=1)[..., None]
    return vals.transpose(0, 1, 3, 2).reshape(g * 512, n)


def gelu(v):
    return 0.5 * v * (1.0 + np.tanh(np.sqrt(2.0 / np.pi) * (v + 0.044715 * v**3)))


def striped8(idx):
    return np.concatenate([v.reshape(-1, 16).T for v in idx]).astype(np.uint16)


def unstriped8(offs):
    return np.stack([offs[16 * g:16 * g + 16].T.reshape(-1) for g in range(8)]).astype(np.int64)


def runs(v, idx8):
    k = np.arange(v.shape[0])
    return v[k[:, None], idx8[k % 512 // 64]]


K, K2, H, N, T, S, T2 = 1024, 512, 1024, 512, 2048, 1024, 2048

def setup_inputs():
    n = np.random.standard_normal
    s = mx_kscale(K)[:, None]
    s2 = mx_kscale(K2)[:, None]
    u = mx_kscale(H)[:, None]
    tab_words, tab_scales = pack_weight(n((K, T)) * s, "e4m3")
    tab2_words, tab2_scales = pack_weight(n((K2, T)) * s2, "e4m3")
    w2_words, w2_scales = pack_weight(0.9 * n((K2, H)) / np.sqrt(K2) / s2, "e2m1")
    return {
        "tab_words": tab_words, "tab_scales": tab_scales,
        "offs": striped8(np.stack([np.random.permutation(T)[:S] for _ in range(8)])),
        "tab2_words": tab2_words, "tab2_scales": tab2_scales,
        "offs2": striped(np.random.permutation(T)[:S]),
        "offs3": striped(np.random.permutation(T2)[:S]),
        "w1": (0.9 * n((K, H)) / np.sqrt(K) / s).astype(np.float32),
        "w2_words": w2_words, "w2_scales": w2_scales,
        "b": (0.5 * n(H)).astype(np.float32),
        "gain": (np.exp(0.3 * n(H)) * u[:, 0]).astype(np.float32),
        "w3": (n((H, N)) / np.sqrt(H) / u).astype(np.float32),
        "page1": n((N, T2)).astype(np.float32),
        "wgo": np.exp(0.3 * n((128, S))).astype(np.float32),
    }

def reference(tab_words, tab_scales, offs, tab2_words, tab2_scales, offs2, offs3, w1, w2_words, w2_scales, b, gain, w3, page1, wgo):
    v = runs(unpack_weight(tab_words, tab_scales, "e4m3"), unstriped8(offs))
    v2 = unpack_weight(tab2_words, tab2_scales, "e4m3")[:, unstriped(offs2)]
    w2 = unpack_weight(w2_words, w2_scales, "e2m1")
    e = mxq(f64(w1), 0, "e4m3").T @ v + w2.T @ v2
    h = np.tanh(e + f64(b)[:, None]) * f64(gain)[:, None]
    y = mxq(f64(w3), 0, "e4m3").T @ mxq(h, 0, "e4m3")
    out = f64(page1).copy()
    out[:, unstriped(offs3)] = np.tile(f64(wgo), (N // 128, 1)) * y
    return out

@@ -1,0 +1,288 @@
+from contextlib import ExitStack
+
+import concourse.mybir as mybir
+
+K, K2, H, N, T, S, T2 = 1024, 512, 1024, 512, 2048, 1024, 2048
+FLOPS = 2 * S * (K * H + K2 * H + H * N)
+
+F32 = mybir.dt.float32
+BF16 = mybir.dt.bfloat16
+I32 = mybir.dt.int32
+U32 = mybir.dt.uint32
+U16 = mybir.dt.uint16
+U8 = mybir.dt.uint8
+FP8X4 = mybir.dt.float8_e4m3fn_x4
+FP4X4 = mybir.dt.float4_e2m1fn_x4
+MULT = mybir.AluOpType.mult
+TANH = mybir.ActivationFunctionType.Tanh
+COPY = mybir.ActivationFunctionType.Copy
+
+P = 128
+PASS = 512
+HALF = 512
+CHUNK = 256
+CHUNKS = tuple((j0, CHUNK) for j0 in range(0, S, CHUNK))
+
+
+def tile_list_drum_hit_matcher_kernel(
+    tc, tab_words, tab_scales, offs, tab2_words, tab2_scales, offs2, offs3,
+    w1, w2_words, w2_scales, b, gain, w3, page1, wgo, out,
+):
+    nc = tc.nc
+    with ExitStack() as ctx:
+        keep = ctx.enter_context(tc.tile_pool(name="keep", bufs=1))
+        ring = ctx.enter_context(tc.tile_pool(name="ring", bufs=2))
+        yring = ctx.enter_context(tc.tile_pool(name="yring", bufs=4))
+        e_psum = ctx.enter_context(tc.psum_pool(name="e_psum", bufs=5))
+        y_psum = ctx.enter_context(tc.psum_pool(name="y_psum", bufs=3))
+
+        def held(shape, dtype, name):
+            return keep.tile(shape, dtype, name=name, align_bytes=64)
+
+        lists = keep.tile([P, S // 16], U16, name="lists")
+        list2 = keep.tile([P, S // 16], U16, name="list2")
+        list3 = keep.tile([P, S // 16], U16, name="list3")
+
+        tab_sc = held([P, T], U8, "tab_sc")
+        tab2_sc = held([P, T], U8, "tab2_sc")
+        w2_sc_raw = held([P, H], U8, "w2_sc_raw")
+        tab2_sc_in = held([P, T], U8, "tab2_sc_in")
+        nc.gpsimd.memset(tab_sc[:].bitcast(I32), 0)
+        nc.vector.memset(w2_sc_raw[:].bitcast(I32), 0)
+        nc.vector.memset(tab2_sc[:].bitcast(I32), 0)
+        for a in range(2):
+            for s in range(2):
+                nc.gpsimd.dma_start(tab_sc[4 * a + s:P:16, :].bitcast(I32), tab_scales[a, s:16:2, :].bitcast(I32))
+
+        tab_w = [held([P, T], I32, f"tab_w{a}") for a in range(3)]
+        w1_parts = {(0, 0): 1, (1, 0): 1, (0, 1): 1, (1, 1): 2}
+        w1_raw = {
+            (a, blk): [held([P, 4, PASS // parts], F32, f"w1_raw{a}{blk}{x}") for x in range(parts)]
+            for (a, blk), parts in w1_parts.items()
+        }
+        w3_raw = {(hf, blk): held([P, 4, 256], F32, f"w3_raw{hf}{blk}") for hf in range(2) for blk in range(2)}
+        w2_raw = held([P, 2 * H], U8, "w2_raw")
+        bias_t = held([P, 2, 4], F32, "bias_t")
+        gain_t = held([P, 2, 4], F32, "gain_t")
+        wgo_t = held([P, S], F32, "wgo_t")
+        pages = [held([P, T2], F32, f"page{n}") for n in range(4)]
+
+        def load_words(dst, words):
+            nc.sync.dma_start(dst[:], words.rearrange("p t i -> p (t i)").bitcast(I32))
+
+        def load_w1(a, blk):
+            width = PASS // w1_parts[a, blk]
+            for x, part in enumerate(w1_raw[a, blk]):
+                c0 = blk * PASS + x * width
+                rows = w1[a * PASS:(a + 1) * PASS, c0:c0 + width]
+                nc.sync.dma_start(part[:], rows.rearrange("(p i) c -> p i c", i=4))
+
+        def load_w3(hf):
+            for blk in range(2):
+                rows = w3[blk * PASS:(blk + 1) * PASS, hf * 256:(hf + 1) * 256]
+                nc.sync.dma_start(w3_raw[hf, blk][:], rows.rearrange("(p i) c -> p i c", i=4))
+
+        def load_page(n):
+            nc.sync.dma_start(pages[n][:], page1[n * P:(n + 1) * P, :])
+
+        nc.sync.dma_start(lists[:], offs)
+        nc.sync.dma_start(list2[:], offs2)
+        for d in range(4):
+            nc.sync.dma_start(tab2_sc_in[32 * d:32 * d + 4, :].bitcast(I32), tab2_scales[0, 4 * d:4 * d + 4, :].bitcast(I32))
+        load_words(tab_w[0], tab_words[0])
+        load_w1(0, 0)
+        nc.sync.dma_start(bias_t[:], b.rearrange("(k p t) -> p k t", p=P, t=4))
+        nc.sync.dma_start(gain_t[:], gain.rearrange("(k p t) -> p k t", p=P, t=4))
+        nc.sync.dma_start(list3[:], offs3)
+        load_w1(1, 0)
+        nc.sync.dma_start(w2_raw[:].bitcast(I32), w2_words[0].bitcast(I32))
+        load_words(tab_w[1], tab_words[1])
+        load_words(tab_w[2], tab2_words[0])
+        load_w1(0, 1)
+        load_w1(1, 1)
+        load_w3(0)
+        nc.sync.dma_start(wgo_t[:], wgo)
+        load_page(0)
+        load_page(1)
+        load_w3(1)
+        load_page(2)
+        load_page(3)
+
+        for d in range(4):
+            nc.gpsimd.dma_start(w2_sc_raw[32 * d:32 * d + 4, :].bitcast(I32), w2_scales[0, 4 * d:4 * d + 4, :].bitcast(I32))
+        for d in range(4):
+            rows = slice(32 * d, 32 * d + 4)
+            nc.vector.tensor_copy(tab2_sc[rows, :].bitcast(I32), tab2_sc_in[rows, :].bitcast(I32))
+
+        v_sc_got = held([P, S], U8, "v_sc_got")
+        v_sc = held([P, S], U8, "v_sc")
+        v2_sc = held([P, S], U8, "v2_sc")
+        nc.vector.tensor_copy(v_sc_got[:], tab_sc[:].indirect(lists[:]))
+        nc.vector.tensor_copy(v_sc[:].bitcast(I32), v_sc_got[:].bitcast(I32))
+        for a in range(2):
+            for s in range(2):
+                nc.gpsimd.dma_start(
+                    v_sc[4 * a + 2 + s:P:32, :].bitcast(I32), v_sc_got[16 + 4 * a + s:P:32, :].bitcast(I32)
+                )
+
+        v = {(a, 0): held([P, HALF], U32, f"v{a}")[:] for a in range(3)}
+
+        def gather_words(a, hf):
+            offsets = (list2 if a == 2 else lists)[:, hf * HALF // 16:(hf + 1) * HALF // 16]
+            nc.vector.tensor_copy(v[a, hf], tab_w[a][:].bitcast(U32).indirect(offsets))
+
+        w1_q = {key: held([P, PASS], U32, f"w1_q{key[0]}{key[1]}") for key in w1_raw}
+        w1_sc = {key: held([P, PASS], U8, f"w1_sc{key[0]}{key[1]}") for key in w1_raw}
+
+        def quantise_w1(a, blk):
+            if (a, blk) == (1, 1):
+                rounded = keep.tile([P, 4 * PASS], BF16, name="w1_bf_last", tag="shared", align_bytes=64)
+            else:
+                rounded = ring.tile([P, 4 * PASS], BF16, name="w1_bf", align_bytes=64)
+            dealt = rounded[:].rearrange("p (t m i) -> p m i t", t=4, i=4)
+            count = P // w1_parts[a, blk]
+            for x, part in enumerate(w1_raw[a, blk]):
+                nc.scalar.copy(dealt[:, x * count:(x + 1) * count], part[:].rearrange("p i (m t) -> p m i t", t=4))
+            nc.vector.quantize_mx(w1_q[a, blk][:].bitcast(FP8X4), w1_sc[a, blk][:], rounded[:])
+
+        w3_q = [held([P, N], U32, f"w3_q{blk}") for blk in range(2)]
+        w3_sc = [held([P, N], U8, f"w3_sc{blk}") for blk in range(2)]
+
+        def quantise_w3(hf):
+            cols = slice(hf * 256, (hf + 1) * 256)
+            for blk in range(2):
+                rounded3 = ring.tile([P, 4 * 256], BF16, name="w3_bf", align_bytes=64)
+                nc.scalar.copy(
+                    rounded3[:].rearrange("p (c u i) -> p c i u", u=4, i=4),
+                    w3_raw[hf, blk][:].rearrange("p i (c u) -> p c i u", u=4),
+                )
+                nc.vector.quantize_mx(w3_q[blk][:, cols].bitcast(FP8X4), w3_sc[blk][:, cols], rounded3[:])
+
+        gather_words(0, 0)
+        quantise_w1(0, 0)
+        nc.vector.tensor_copy(v2_sc[:], tab2_sc[:].indirect(list2[:]))
+        quantise_w1(1, 0)
+
+        w2_dealt = held([P, 2 * H], U8, "w2_dealt")
+        w2_sc = held([P, H], U8, "w2_sc")
+        nc.scalar.copy(
+            w2_dealt[:].bitcast(U16).rearrange("p (k t m) -> p k t m", k=2, t=4),
+            w2_raw[:].bitcast(U16).rearrange("p (k m t) -> p k t m", k=2, t=4),
+        )
+        nc.vector.tensor_copy(
+            w2_sc[:].rearrange("p (k t m) -> p k t m", k=2, t=4),
+            w2_sc_raw[:].rearrange("p (k m t) -> p k t m", k=2, t=4),
+        )
+        for a in (1, 2):
+            gather_words(a, 0)
+
+        act = {(blk, c): held([P, 4, CHUNKS[c][1]], F32, f"act{blk}{c}") for blk in range(2) for c in range(4)}
+        h_q = [held([P, S], U32, f"h_q{blk}") for blk in range(2)]
+        h_sc = [held([P, S], U8, f"h_sc{blk}") for blk in range(2)]
+
+        def e_pass(bank, blk, t, hf, a, start, stop):
+            cols = slice(hf * HALF, (hf + 1) * HALF)
+            if a == 2:
+                r0 = blk * PASS + t * P
+                lhs, lhs_sc = w2_dealt[:, 2 * r0:2 * (r0 + P)].bitcast(FP4X4), w2_sc[:, r0:r0 + P]
+                rhs_sc = v2_sc[:, cols]
+            else:
+                lhs, lhs_sc = w1_q[a, blk][:, t * P:(t + 1) * P].bitcast(FP8X4), w1_sc[a, blk][:, t * P:(t + 1) * P]
+                rhs_sc = v_sc[4 * a:P, cols]
+            nc.tensor.matmul_mx(bank[:], lhs, lhs_sc, v[a, hf].bitcast(FP8X4), rhs_sc, start=start, stop=stop)
+
+        def first_stage(blk, hf, order):
+            banks = [e_psum.tile([P, HALF], F32, name="e_bank") for t in range(4)]
+            for t in range(4):
+                e_pass(banks[t], blk, t, hf, order[0], True, False)
+                e_pass(banks[t], blk, t, hf, order[1], False, False)
+            for t in range(4):
+                e_pass(banks[t], blk, t, hf, order[2], False, True)
+            for c, (j0, width) in enumerate(CHUNKS):
+                if j0 // HALF == hf:
+                    for t in range(4):
+                        nc.scalar.activation(
+                            act[blk, c][:, t, :], banks[t][:, j0 % HALF:j0 % HALF + width], TANH,
+                            bias=bias_t[:, blk, t:t + 1],
+                        )
+
+        def apply_gain(blk, c):
+            j0, width = CHUNKS[c]
+            h_bf = held([P, 4 * width], BF16, f"h_bf{blk}{c}")
+            gains = gain_t[:, blk, :].rearrange("p (c t u) -> p c t u", c=1, u=1).to_broadcast([P, width // 4, 4, 4])
+            nc.vector.tensor_tensor(
+                h_bf[:].rearrange("p (c u t) -> p c t u", u=4, t=4),
+                act[blk, c][:].rearrange("p t (c u) -> p c t u", u=4),
+                gains, MULT,
+            )
+            return h_bf
+
+        def apply_gain_scalar(blk, c):
+            j0, width = CHUNKS[c]
+            planes = ring.tile([P, 4, width], BF16, name="h_planes", align_bytes=64)
+            for t in range(4):
+                nc.scalar.activation(planes[:, t, :], act[blk, c][:, t, :], COPY, scale=gain_t[:, blk, t:t + 1])
+            h_bf = held([P, 4 * width], BF16, f"h_bf{blk}{c}")
+            nc.scalar.copy(
+                h_bf[:].rearrange("p (c u t) -> p c t u", u=4, t=4),
+                planes[:].rearrange("p t (c u) -> p c t u", u=4),
+            )
+            return h_bf
+
+        def quantise_h(blk, c, h_bf):
+            j0, width = CHUNKS[c]
+            nc.vector.quantize_mx(h_q[blk][:, j0:j0 + width].bitcast(FP8X4), h_sc[blk][:, j0:j0 + width], h_bf[:])
+
+        def second_stage(n, j0, width):
+            bank = y_psum.tile([P, HALF], F32, name="y_bank")
+            rows, cols = slice(n * P, (n + 1) * P), slice(j0, j0 + width)
+            for blk in range(2):
+                nc.tensor.matmul_mx(
+                    bank[:, 0:width], w3_q[blk][:, rows].bitcast(FP8X4), w3_sc[blk][:, rows],
+                    h_q[blk][:, cols].bitcast(FP8X4), h_sc[blk][:, cols], start=(blk == 0), stop=(blk == 1),
+                )
+            y = yring.tile([P, HALF], F32, name="y")
+            nc.scalar.copy(y[:, 0:width], bank[:, 0:width])
+            nc.vector.tensor_tensor(
+                pages[n][:].indirect(list3[:, j0 // 16:(j0 + width) // 16]), y[:, 0:width], wgo_t[:, cols], MULT
+            )
+
+        def store(n):
+            nc.sync.dma_start(out[n * P:(n + 1) * P, :], pages[n][:])
+
+        first_stage(0, 0, (0, 1, 2))
+        quantise_w1(0, 1)
+        h00, h01 = apply_gain(0, 0), apply_gain(0, 1)
+        quantise_h(0, 0, h00)
+        quantise_h(0, 1, h01)
+        quantise_w1(1, 1)
+        v_late = keep.tile([P, 3 * HALF], U32, name="v_late", tag="shared", align_bytes=64)
+        for a in range(3):
+            v[a, 1] = v_late[:, a * HALF:(a + 1) * HALF]
+            gather_words(a, 1)
+        first_stage(1, 0, (0, 2, 1))
+        quantise_w3(0)
+        h10 = apply_gain(1, 0)
+        quantise_h(1, 0, h10)
+        second_stage(0, 0, 256)
+        h11 = apply_gain(1, 1)
+        second_stage(1, 0, 256)
+        quantise_h(1, 1, h11)
+        first_stage(0, 1, (0, 1, 2))
+        first_stage(1, 1, (0, 2, 1))
+        second_stage(0, 256, 256)
+        second_stage(1, 256, 256)
+        quantise_w3(1)
+        second_stage(2, 0, 512)
+        second_stage(3, 0, 512)
+        for c in (2, 3):
+            for blk in range(2):
+                quantise_h(blk, c, apply_gain_scalar(blk, c))
+        second_stage(0, 512, 256)
+        second_stage(1, 512, 256)
+        for n in range(4):
+            second_stage(n, 768, 256)
+            if n < 2:
+                second_stage(n + 2, 512, 256)
+        for n in range(4):
+            store(n)

@@ -32,9 +32,9 @@ def tile_list_drum_hit_matcher_kernel(
     with ExitStack() as ctx:
         keep = ctx.enter_context(tc.tile_pool(name="keep", bufs=1))
         ring = ctx.enter_context(tc.tile_pool(name="ring", bufs=2))
-        yring = ctx.enter_context(tc.tile_pool(name="yring", bufs=4))
-        e_psum = ctx.enter_context(tc.psum_pool(name="e_psum", bufs=5))
-        y_psum = ctx.enter_context(tc.psum_pool(name="y_psum", bufs=3))
+        yring = ctx.enter_context(tc.tile_pool(name="yring", bufs=6))
+        e_psum = ctx.enter_context(tc.psum_pool(name="e_psum", bufs=6))
+        y_psum = ctx.enter_context(tc.psum_pool(name="y_psum", bufs=2))
 
         def held(shape, dtype, name):
             return keep.tile(shape, dtype, name=name, align_bytes=64)
@@ -43,19 +43,16 @@ def tile_list_drum_hit_matcher_kernel(
         list2 = keep.tile([P, S // 16], U16, name="list2")
         list3 = keep.tile([P, S // 16], U16, name="list3")
 
-        tab_sc = held([P, T], U8, "tab_sc")
+        tab_sc = keep.tile([P, T], U8, name="tab_sc", tag="scale_window", align_bytes=64)
         tab2_sc = held([P, T], U8, "tab2_sc")
         w2_sc_raw = held([P, H], U8, "w2_sc_raw")
         tab2_sc_in = held([P, T], U8, "tab2_sc_in")
-        nc.gpsimd.memset(tab_sc[:].bitcast(I32), 0)
-        nc.vector.memset(w2_sc_raw[:].bitcast(I32), 0)
+        nc.gpsimd.memset(w2_sc_raw[:].bitcast(I32), 0)
+        nc.vector.memset(tab_sc[:].bitcast(I32), 0)
         nc.vector.memset(tab2_sc[:].bitcast(I32), 0)
-        for a in range(2):
-            for s in range(2):
-                nc.gpsimd.dma_start(tab_sc[4 * a + s:P:16, :].bitcast(I32), tab_scales[a, s:16:2, :].bitcast(I32))
 
         tab_w = [held([P, T], I32, f"tab_w{a}") for a in range(3)]
-        w1_parts = {(0, 0): 1, (1, 0): 1, (0, 1): 1, (1, 1): 2}
+        w1_parts = {(0, 0): 1, (1, 0): 1, (0, 1): 1, (1, 1): 1}
         w1_raw = {
             (a, blk): [held([P, 4, PASS // parts], F32, f"w1_raw{a}{blk}{x}") for x in range(parts)]
             for (a, blk), parts in w1_parts.items()
@@ -91,16 +88,38 @@ def tile_list_drum_hit_matcher_kernel(
             nc.sync.dma_start(tab2_sc_in[32 * d:32 * d + 4, :].bitcast(I32), tab2_scales[0, 4 * d:4 * d + 4, :].bitcast(I32))
         load_words(tab_w[0], tab_words[0])
         load_w1(0, 0)
-        nc.sync.dma_start(bias_t[:], b.rearrange("(k p t) -> p k t", p=P, t=4))
-        nc.sync.dma_start(gain_t[:], gain.rearrange("(k p t) -> p k t", p=P, t=4))
-        nc.sync.dma_start(list3[:], offs3)
+        for a in range(2):
+            for s in range(2):
+                nc.sync.dma_start(tab_sc[4 * a + s:P:16, :].bitcast(I32), tab_scales[a, s:16:2, :].bitcast(I32))
         load_w1(1, 0)
         nc.sync.dma_start(w2_raw[:].bitcast(I32), w2_words[0].bitcast(I32))
         load_words(tab_w[1], tab_words[1])
-        load_words(tab_w[2], tab2_words[0])
         load_w1(0, 1)
-        load_w1(1, 1)
+        for d in range(4):
+            nc.sync.dma_start(w2_sc_raw[32 * d:32 * d + 4, :].bitcast(I32), w2_scales[0, 4 * d:4 * d + 4, :].bitcast(I32))
+
+
+        for d in range(4):
+            rows = slice(32 * d, 32 * d + 4)
+            nc.vector.tensor_copy(tab2_sc[rows, :].bitcast(I32), tab2_sc_in[rows, :].bitcast(I32))
+
+        v_sc_got = held([P, S], U8, "v_sc_got")
+        v_sc = held([P, S], U8, "v_sc")
+        nc.vector.tensor_copy(v_sc_got[:], tab_sc[:].indirect(lists[:]))
+        nc.vector.tensor_copy(v_sc[:].bitcast(I32), v_sc_got[:].bitcast(I32))
+        for a in range(2):
+            for s in range(2):
+                nc.sync.dma_start(
+                    v_sc[4 * a + 2 + s:P:32, :].bitcast(I32), v_sc_got[16 + 4 * a + s:P:32, :].bitcast(I32)
+                )
+            if a == 0:
+                load_w1(1, 1)
+
+        load_words(tab_w[2], tab2_words[0])
+        nc.sync.dma_start(bias_t[:], b.rearrange("(k p t) -> p k t", p=P, t=4))
+        nc.sync.dma_start(gain_t[:], gain.rearrange("(k p t) -> p k t", p=P, t=4))
         load_w3(0)
+        nc.sync.dma_start(list3[:], offs3)
         nc.sync.dma_start(wgo_t[:], wgo)
         load_page(0)
         load_page(1)
@@ -108,58 +127,39 @@ def tile_list_drum_hit_matcher_kernel(
         load_page(2)
         load_page(3)
 
-        for d in range(4):
-            nc.gpsimd.dma_start(w2_sc_raw[32 * d:32 * d + 4, :].bitcast(I32), w2_scales[0, 4 * d:4 * d + 4, :].bitcast(I32))
-        for d in range(4):
-            rows = slice(32 * d, 32 * d + 4)
-            nc.vector.tensor_copy(tab2_sc[rows, :].bitcast(I32), tab2_sc_in[rows, :].bitcast(I32))
+        v = [held([P, S], U32, f"v{a}") for a in range(3)]
 
-        v_sc_got = held([P, S], U8, "v_sc_got")
-        v_sc = held([P, S], U8, "v_sc")
-        v2_sc = held([P, S], U8, "v2_sc")
-        nc.vector.tensor_copy(v_sc_got[:], tab_sc[:].indirect(lists[:]))
-        nc.vector.tensor_copy(v_sc[:].bitcast(I32), v_sc_got[:].bitcast(I32))
-        for a in range(2):
-            for s in range(2):
-                nc.gpsimd.dma_start(
-                    v_sc[4 * a + 2 + s:P:32, :].bitcast(I32), v_sc_got[16 + 4 * a + s:P:32, :].bitcast(I32)
-                )
-
-        v = {(a, 0): held([P, HALF], U32, f"v{a}")[:] for a in range(3)}
-
-        def gather_words(a, hf):
-            offsets = (list2 if a == 2 else lists)[:, hf * HALF // 16:(hf + 1) * HALF // 16]
-            nc.vector.tensor_copy(v[a, hf], tab_w[a][:].bitcast(U32).indirect(offsets))
+        def gather_words(a, j0, width):
+            offsets = (list2 if a == 2 else lists)[:, j0 // 16:(j0 + width) // 16]
+            nc.vector.tensor_copy(v[a][:, j0:j0 + width], tab_w[a][:].bitcast(U32).indirect(offsets))
 
         w1_q = {key: held([P, PASS], U32, f"w1_q{key[0]}{key[1]}") for key in w1_raw}
         w1_sc = {key: held([P, PASS], U8, f"w1_sc{key[0]}{key[1]}") for key in w1_raw}
 
         def quantise_w1(a, blk):
-            if (a, blk) == (1, 1):
-                rounded = keep.tile([P, 4 * PASS], BF16, name="w1_bf_last", tag="shared", align_bytes=64)
-            else:
-                rounded = ring.tile([P, 4 * PASS], BF16, name="w1_bf", align_bytes=64)
+            rounded = ring.tile([P, 4 * PASS], BF16, name="w1_bf", align_bytes=64)
             dealt = rounded[:].rearrange("p (t m i) -> p m i t", t=4, i=4)
             count = P // w1_parts[a, blk]
             for x, part in enumerate(w1_raw[a, blk]):
                 nc.scalar.copy(dealt[:, x * count:(x + 1) * count], part[:].rearrange("p i (m t) -> p m i t", t=4))
             nc.vector.quantize_mx(w1_q[a, blk][:].bitcast(FP8X4), w1_sc[a, blk][:], rounded[:])
 
-        w3_q = [held([P, N], U32, f"w3_q{blk}") for blk in range(2)]
-        w3_sc = [held([P, N], U8, f"w3_sc{blk}") for blk in range(2)]
+        w3_q = [held([P, 2 * P], U32, f"w3_q{n}") for n in range(4)]
+        w3_sc = [held([P, 2 * P], U8, f"w3_sc{n}") for n in range(4)]
 
-        def quantise_w3(hf):
-            cols = slice(hf * 256, (hf + 1) * 256)
+        def quantise_w3(n):
+            rounded3 = ring.tile([P, 2 * 4 * P], BF16, name="w3_bf", align_bytes=64)
             for blk in range(2):
-                rounded3 = ring.tile([P, 4 * 256], BF16, name="w3_bf", align_bytes=64)
+                raw = w3_raw[n // 2, blk][:, :, n % 2 * P:(n % 2 + 1) * P]
                 nc.scalar.copy(
-                    rounded3[:].rearrange("p (c u i) -> p c i u", u=4, i=4),
-                    w3_raw[hf, blk][:].rearrange("p i (c u) -> p c i u", u=4),
+                    rounded3[:, blk * 4 * P:(blk + 1) * 4 * P].rearrange("p (c u i) -> p c i u", u=4, i=4),
+                    raw.rearrange("p i (c u) -> p c i u", u=4),
                 )
-                nc.vector.quantize_mx(w3_q[blk][:, cols].bitcast(FP8X4), w3_sc[blk][:, cols], rounded3[:])
+            nc.vector.quantize_mx(w3_q[n][:].bitcast(FP8X4), w3_sc[n][:], rounded3[:])
 
-        gather_words(0, 0)
+        gather_words(0, 0, S)
         quantise_w1(0, 0)
+        v2_sc = keep.tile([P, S], U8, name="v2_sc", tag="scale_window", align_bytes=64)
         nc.vector.tensor_copy(v2_sc[:], tab2_sc[:].indirect(list2[:]))
         quantise_w1(1, 0)
 
@@ -173,15 +173,25 @@ def tile_list_drum_hit_matcher_kernel(
             w2_sc[:].rearrange("p (k t m) -> p k t m", k=2, t=4),
             w2_sc_raw[:].rearrange("p (k m t) -> p k t m", k=2, t=4),
         )
-        for a in (1, 2):
-            gather_words(a, 0)
+        gather_words(1, 0, S)
+        quantise_w1(0, 1)
+        quantise_w1(1, 1)
+        gather_words(2, 0, CHUNK)
+        gather_words(2, CHUNK, CHUNK)
+        gather_words(2, HALF, HALF)
 
-        act = {(blk, c): held([P, 4, CHUNKS[c][1]], F32, f"act{blk}{c}") for blk in range(2) for c in range(4)}
+        spans = ((0, CHUNK), (CHUNK, CHUNK), (HALF, HALF))
+        act = {(blk, j0): held([P, 4, width], F32, f"act{blk}_{j0}") for blk in range(2) for j0, width in spans}
+
+        def act_cols(blk, j0, width):
+            base = min(j0, HALF)
+            return act[blk, base][:, :, j0 - base:j0 - base + width]
+
         h_q = [held([P, S], U32, f"h_q{blk}") for blk in range(2)]
         h_sc = [held([P, S], U8, f"h_sc{blk}") for blk in range(2)]
 
-        def e_pass(bank, blk, t, hf, a, start, stop):
-            cols = slice(hf * HALF, (hf + 1) * HALF)
+        def e_pass(sums, blk, t, j0, width, a, start, stop):
+            cols = slice(j0, j0 + width)
             if a == 2:
                 r0 = blk * PASS + t * P
                 lhs, lhs_sc = w2_dealt[:, 2 * r0:2 * (r0 + P)].bitcast(FP4X4), w2_sc[:, r0:r0 + P]
@@ -189,22 +199,29 @@ def tile_list_drum_hit_matcher_kernel(
             else:
                 lhs, lhs_sc = w1_q[a, blk][:, t * P:(t + 1) * P].bitcast(FP8X4), w1_sc[a, blk][:, t * P:(t + 1) * P]
                 rhs_sc = v_sc[4 * a:P, cols]
-            nc.tensor.matmul_mx(bank[:], lhs, lhs_sc, v[a, hf].bitcast(FP8X4), rhs_sc, start=start, stop=stop)
+            nc.tensor.matmul_mx(sums, lhs, lhs_sc, v[a][:, cols].bitcast(FP8X4), rhs_sc, start=start, stop=stop)
 
-        def first_stage(blk, hf, order):
-            banks = [e_psum.tile([P, HALF], F32, name="e_bank") for t in range(4)]
-            for t in range(4):
-                e_pass(banks[t], blk, t, hf, order[0], True, False)
-                e_pass(banks[t], blk, t, hf, order[1], False, False)
-            for t in range(4):
-                e_pass(banks[t], blk, t, hf, order[2], False, True)
-            for c, (j0, width) in enumerate(CHUNKS):
-                if j0 // HALF == hf:
+        def first_stage(blks, j0, width):
+            per_bank = HALF // width
+            banks = {
+                (blk, u): e_psum.tile([P, HALF], F32, name="e_bank") for blk in blks for u in range(4 // per_bank)
+            }
+
+            def sums(blk, t):
+                c0 = t % per_bank * width
+                return banks[blk, t // per_bank][:, c0:c0 + width]
+
+            for blk in blks:
+                for a in range(2):
                     for t in range(4):
-                        nc.scalar.activation(
-                            act[blk, c][:, t, :], banks[t][:, j0 % HALF:j0 % HALF + width], TANH,
-                            bias=bias_t[:, blk, t:t + 1],
-                        )
+                        e_pass(sums(blk, t), blk, t, j0, width, a, a == 0 and t % per_bank == 0, False)
+            for blk in blks:
+                for t in range(4):
+                    e_pass(sums(blk, t), blk, t, j0, width, 2, False, t % per_bank == per_bank - 1)
+                for t in range(4):
+                    nc.scalar.activation(
+                        act[blk, j0][:, t, :], sums(blk, t), TANH, bias=bias_t[:, blk, t:t + 1]
+                    )
 
         def apply_gain(blk, c):
             j0, width = CHUNKS[c]
@@ -212,16 +229,16 @@ def tile_list_drum_hit_matcher_kernel(
             gains = gain_t[:, blk, :].rearrange("p (c t u) -> p c t u", c=1, u=1).to_broadcast([P, width // 4, 4, 4])
             nc.vector.tensor_tensor(
                 h_bf[:].rearrange("p (c u t) -> p c t u", u=4, t=4),
-                act[blk, c][:].rearrange("p t (c u) -> p c t u", u=4),
+                act_cols(blk, j0, width).rearrange("p t (c u) -> p c t u", u=4),
                 gains, MULT,
             )
             return h_bf
 
         def apply_gain_scalar(blk, c):
             j0, width = CHUNKS[c]
-            planes = ring.tile([P, 4, width], BF16, name="h_planes", align_bytes=64)
+            planes = keep.tile([P, 4, width], BF16, name="h_planes", tag=f"planes{blk}{c}", align_bytes=64)
             for t in range(4):
-                nc.scalar.activation(planes[:, t, :], act[blk, c][:, t, :], COPY, scale=gain_t[:, blk, t:t + 1])
+                nc.scalar.activation(planes[:, t, :], act_cols(blk, j0, width)[:, t, :], COPY, scale=gain_t[:, blk, t:t + 1])
             h_bf = held([P, 4 * width], BF16, f"h_bf{blk}{c}")
             nc.scalar.copy(
                 h_bf[:].rearrange("p (c u t) -> p c t u", u=4, t=4),
@@ -233,15 +250,19 @@ def tile_list_drum_hit_matcher_kernel(
             j0, width = CHUNKS[c]
             nc.vector.quantize_mx(h_q[blk][:, j0:j0 + width].bitcast(FP8X4), h_sc[blk][:, j0:j0 + width], h_bf[:])
 
-        def second_stage(n, j0, width):
+        def second_stage(n, j0, width, after=None):
             bank = y_psum.tile([P, HALF], F32, name="y_bank")
-            rows, cols = slice(n * P, (n + 1) * P), slice(j0, j0 + width)
+            cols = slice(j0, j0 + width)
             for blk in range(2):
+                rows = slice(blk * P, (blk + 1) * P)
                 nc.tensor.matmul_mx(
-                    bank[:, 0:width], w3_q[blk][:, rows].bitcast(FP8X4), w3_sc[blk][:, rows],
+                    bank[:, 0:width], w3_q[n][:, rows].bitcast(FP8X4), w3_sc[n][:, rows],
                     h_q[blk][:, cols].bitcast(FP8X4), h_sc[blk][:, cols], start=(blk == 0), stop=(blk == 1),
                 )
-            y = yring.tile([P, HALF], F32, name="y")
+            if after is None:
+                y = yring.tile([P, HALF], F32, name="y")
+            else:
+                y = keep.tile([P, HALF], F32, name="y_held", tag=after, align_bytes=64)
             nc.scalar.copy(y[:, 0:width], bank[:, 0:width])
             nc.vector.tensor_tensor(
                 pages[n][:].indirect(list3[:, j0 // 16:(j0 + width) // 16]), y[:, 0:width], wgo_t[:, cols], MULT
@@ -250,39 +271,34 @@ def tile_list_drum_hit_matcher_kernel(
         def store(n):
             nc.sync.dma_start(out[n * P:(n + 1) * P, :], pages[n][:])
 
-        first_stage(0, 0, (0, 1, 2))
-        quantise_w1(0, 1)
-        h00, h01 = apply_gain(0, 0), apply_gain(0, 1)
-        quantise_h(0, 0, h00)
-        quantise_h(0, 1, h01)
-        quantise_w1(1, 1)
-        v_late = keep.tile([P, 3 * HALF], U32, name="v_late", tag="shared", align_bytes=64)
-        for a in range(3):
-            v[a, 1] = v_late[:, a * HALF:(a + 1) * HALF]
-            gather_words(a, 1)
-        first_stage(1, 0, (0, 2, 1))
+        first_stage((0, 1), 0, CHUNK)
+        for blk in range(2):
+            quantise_h(blk, 0, apply_gain(blk, 0))
         quantise_w3(0)
-        h10 = apply_gain(1, 0)
-        quantise_h(1, 0, h10)
-        second_stage(0, 0, 256)
-        h11 = apply_gain(1, 1)
-        second_stage(1, 0, 256)
-        quantise_h(1, 1, h11)
-        first_stage(0, 1, (0, 1, 2))
-        first_stage(1, 1, (0, 2, 1))
-        second_stage(0, 256, 256)
-        second_stage(1, 256, 256)
+        second_stage(0, 0, CHUNK)
+        first_stage((0,), CHUNK, CHUNK)
         quantise_w3(1)
-        second_stage(2, 0, 512)
-        second_stage(3, 0, 512)
-        for c in (2, 3):
-            for blk in range(2):
-                quantise_h(blk, c, apply_gain_scalar(blk, c))
-        second_stage(0, 512, 256)
-        second_stage(1, 512, 256)
-        for n in range(4):
-            second_stage(n, 768, 256)
-            if n < 2:
-                second_stage(n + 2, 512, 256)
-        for n in range(4):
+        second_stage(1, 0, CHUNK)
+        first_stage((1,), CHUNK, CHUNK)
+        for blk in range(2):
+            quantise_h(blk, 1, apply_gain(blk, 1))
+        quantise_w3(2)
+        second_stage(2, 0, CHUNK)
+        for n in range(3):
+            second_stage(n, CHUNK, CHUNK)
+        first_stage((0,), HALF, HALF)
+        first_stage((1,), HALF, HALF)
+        quantise_w3(3)
+        quantise_h(0, 2, apply_gain(0, 2))
+        quantise_h(1, 2, apply_gain_scalar(1, 2))
+        second_stage(3, 0, HALF, after="planes12")
+        second_stage(0, HALF, CHUNK)
+        for blk in range(2):
+            quantise_h(blk, 3, apply_gain_scalar(blk, 3))
+        second_stage(1, HALF, CHUNK, after="planes13")
+        second_stage(2, HALF, CHUNK)
+        for n in range(3):
+            second_stage(n, HALF + CHUNK, CHUNK)
             store(n)
+        second_stage(3, HALF, HALF)
+        store(3)

@@ -21,7 +21,10 @@ P = 128
 PASS = 512
 HALF = 512
 CHUNK = 256
-CHUNKS = tuple((j0, CHUNK) for j0 in range(0, S, CHUNK))
+W3_COLS = 256
+TAB2 = 2
+Y_BUFS = 6
+E_BANKS, Y_BANKS = 6, 2
 
 
 def tile_list_drum_hit_matcher_kernel(
@@ -32,9 +35,9 @@ def tile_list_drum_hit_matcher_kernel(
     with ExitStack() as ctx:
         keep = ctx.enter_context(tc.tile_pool(name="keep", bufs=1))
         ring = ctx.enter_context(tc.tile_pool(name="ring", bufs=2))
-        yring = ctx.enter_context(tc.tile_pool(name="yring", bufs=6))
-        e_psum = ctx.enter_context(tc.psum_pool(name="e_psum", bufs=6))
-        y_psum = ctx.enter_context(tc.psum_pool(name="y_psum", bufs=2))
+        yring = ctx.enter_context(tc.tile_pool(name="yring", bufs=Y_BUFS))
+        e_psum = ctx.enter_context(tc.psum_pool(name="e_psum", bufs=E_BANKS))
+        y_psum = ctx.enter_context(tc.psum_pool(name="y_psum", bufs=Y_BANKS))
 
         def held(shape, dtype, name):
             return keep.tile(shape, dtype, name=name, align_bytes=64)
@@ -52,12 +55,8 @@ def tile_list_drum_hit_matcher_kernel(
         nc.vector.memset(tab2_sc[:].bitcast(I32), 0)
 
         tab_w = [held([P, T], I32, f"tab_w{a}") for a in range(3)]
-        w1_parts = {(0, 0): 1, (1, 0): 1, (0, 1): 1, (1, 1): 1}
-        w1_raw = {
-            (a, blk): [held([P, 4, PASS // parts], F32, f"w1_raw{a}{blk}{x}") for x in range(parts)]
-            for (a, blk), parts in w1_parts.items()
-        }
-        w3_raw = {(hf, blk): held([P, 4, 256], F32, f"w3_raw{hf}{blk}") for hf in range(2) for blk in range(2)}
+        w1_raw = {(a, blk): held([P, 4, PASS], F32, f"w1_raw{a}{blk}") for blk in range(2) for a in range(2)}
+        w3_raw = {(hf, blk): held([P, 4, W3_COLS], F32, f"w3_raw{hf}{blk}") for hf in range(2) for blk in range(2)}
         w2_raw = held([P, 2 * H], U8, "w2_raw")
         bias_t = held([P, 2, 4], F32, "bias_t")
         gain_t = held([P, 2, 4], F32, "gain_t")
@@ -67,26 +66,26 @@ def tile_list_drum_hit_matcher_kernel(
         def load_words(dst, words):
             nc.sync.dma_start(dst[:], words.rearrange("p t i -> p (t i)").bitcast(I32))
 
+        def load_scale_rows(dst, scales):
+            for d in range(4):
+                nc.sync.dma_start(dst[32 * d:32 * d + 4, :].bitcast(I32), scales[4 * d:4 * d + 4, :].bitcast(I32))
+
         def load_w1(a, blk):
-            width = PASS // w1_parts[a, blk]
-            for x, part in enumerate(w1_raw[a, blk]):
-                c0 = blk * PASS + x * width
-                rows = w1[a * PASS:(a + 1) * PASS, c0:c0 + width]
-                nc.sync.dma_start(part[:], rows.rearrange("(p i) c -> p i c", i=4))
+            rows = w1[a * PASS:(a + 1) * PASS, blk * PASS:(blk + 1) * PASS]
+            nc.sync.dma_start(w1_raw[a, blk][:], rows.rearrange("(p i) c -> p i c", i=4))
 
         def load_w3(hf):
             for blk in range(2):
-                rows = w3[blk * PASS:(blk + 1) * PASS, hf * 256:(hf + 1) * 256]
+                rows = w3[blk * PASS:(blk + 1) * PASS, hf * W3_COLS:(hf + 1) * W3_COLS]
                 nc.sync.dma_start(w3_raw[hf, blk][:], rows.rearrange("(p i) c -> p i c", i=4))
 
         def load_page(n):
             nc.sync.dma_start(pages[n][:], page1[n * P:(n + 1) * P, :])
 
         nc.sync.dma_start(lists[:], offs)
-        nc.sync.dma_start(list2[:], offs2)
-        for d in range(4):
-            nc.sync.dma_start(tab2_sc_in[32 * d:32 * d + 4, :].bitcast(I32), tab2_scales[0, 4 * d:4 * d + 4, :].bitcast(I32))
         load_words(tab_w[0], tab_words[0])
+        nc.sync.dma_start(list2[:], offs2)
+        load_scale_rows(tab2_sc_in, tab2_scales[0])
         load_w1(0, 0)
         for a in range(2):
             for s in range(2):
@@ -95,29 +94,30 @@ def tile_list_drum_hit_matcher_kernel(
         nc.sync.dma_start(w2_raw[:].bitcast(I32), w2_words[0].bitcast(I32))
         load_words(tab_w[1], tab_words[1])
         load_w1(0, 1)
-        for d in range(4):
-            nc.sync.dma_start(w2_sc_raw[32 * d:32 * d + 4, :].bitcast(I32), w2_scales[0, 4 * d:4 * d + 4, :].bitcast(I32))
-
+        load_scale_rows(w2_sc_raw, w2_scales[0])
 
         for d in range(4):
-            rows = slice(32 * d, 32 * d + 4)
-            nc.vector.tensor_copy(tab2_sc[rows, :].bitcast(I32), tab2_sc_in[rows, :].bitcast(I32))
+            quadrant = slice(32 * d, 32 * d + 4)
+            nc.vector.tensor_copy(tab2_sc[quadrant, :].bitcast(I32), tab2_sc_in[quadrant, :].bitcast(I32))
 
         v_sc_got = held([P, S], U8, "v_sc_got")
         v_sc = held([P, S], U8, "v_sc")
         nc.vector.tensor_copy(v_sc_got[:], tab_sc[:].indirect(lists[:]))
         nc.vector.tensor_copy(v_sc[:].bitcast(I32), v_sc_got[:].bitcast(I32))
-        for a in range(2):
+
+        def move_odd_rows(a):
             for s in range(2):
                 nc.sync.dma_start(
                     v_sc[4 * a + 2 + s:P:32, :].bitcast(I32), v_sc_got[16 + 4 * a + s:P:32, :].bitcast(I32)
                 )
-            if a == 0:
-                load_w1(1, 1)
 
-        load_words(tab_w[2], tab2_words[0])
-        nc.sync.dma_start(bias_t[:], b.rearrange("(k p t) -> p k t", p=P, t=4))
-        nc.sync.dma_start(gain_t[:], gain.rearrange("(k p t) -> p k t", p=P, t=4))
+        move_odd_rows(0)
+        load_w1(1, 1)
+        move_odd_rows(1)
+
+        load_words(tab_w[TAB2], tab2_words[0])
+        nc.sync.dma_start(bias_t[:], b.rearrange("(blk p t) -> p blk t", p=P, t=4))
+        nc.sync.dma_start(gain_t[:], gain.rearrange("(blk p t) -> p blk t", p=P, t=4))
         load_w3(0)
         nc.sync.dma_start(list3[:], offs3)
         nc.sync.dma_start(wgo_t[:], wgo)
@@ -130,32 +130,32 @@ def tile_list_drum_hit_matcher_kernel(
         v = [held([P, S], U32, f"v{a}") for a in range(3)]
 
         def gather_words(a, j0, width):
-            offsets = (list2 if a == 2 else lists)[:, j0 // 16:(j0 + width) // 16]
+            offsets = (list2 if a == TAB2 else lists)[:, j0 // 16:(j0 + width) // 16]
             nc.vector.tensor_copy(v[a][:, j0:j0 + width], tab_w[a][:].bitcast(U32).indirect(offsets))
 
-        w1_q = {key: held([P, PASS], U32, f"w1_q{key[0]}{key[1]}") for key in w1_raw}
-        w1_sc = {key: held([P, PASS], U8, f"w1_sc{key[0]}{key[1]}") for key in w1_raw}
+        w1_q = {(a, blk): held([P, PASS], U32, f"w1_q{a}{blk}") for a, blk in w1_raw}
+        w1_sc = {(a, blk): held([P, PASS], U8, f"w1_sc{a}{blk}") for a, blk in w1_raw}
 
         def quantise_w1(a, blk):
-            rounded = ring.tile([P, 4 * PASS], BF16, name="w1_bf", align_bytes=64)
-            dealt = rounded[:].rearrange("p (t m i) -> p m i t", t=4, i=4)
-            count = P // w1_parts[a, blk]
-            for x, part in enumerate(w1_raw[a, blk]):
-                nc.scalar.copy(dealt[:, x * count:(x + 1) * count], part[:].rearrange("p i (m t) -> p m i t", t=4))
-            nc.vector.quantize_mx(w1_q[a, blk][:].bitcast(FP8X4), w1_sc[a, blk][:], rounded[:])
+            w1_bf = ring.tile([P, 4 * PASS], BF16, name="w1_bf", align_bytes=64)
+            nc.scalar.copy(
+                w1_bf[:].rearrange("p (t m i) -> p m i t", t=4, i=4),
+                w1_raw[a, blk][:].rearrange("p i (m t) -> p m i t", t=4),
+            )
+            nc.vector.quantize_mx(w1_q[a, blk][:].bitcast(FP8X4), w1_sc[a, blk][:], w1_bf[:])
 
         w3_q = [held([P, 2 * P], U32, f"w3_q{n}") for n in range(4)]
         w3_sc = [held([P, 2 * P], U8, f"w3_sc{n}") for n in range(4)]
 
         def quantise_w3(n):
-            rounded3 = ring.tile([P, 2 * 4 * P], BF16, name="w3_bf", align_bytes=64)
+            w3_bf = ring.tile([P, 2 * 4 * P], BF16, name="w3_bf", align_bytes=64)
             for blk in range(2):
                 raw = w3_raw[n // 2, blk][:, :, n % 2 * P:(n % 2 + 1) * P]
                 nc.scalar.copy(
-                    rounded3[:, blk * 4 * P:(blk + 1) * 4 * P].rearrange("p (c u i) -> p c i u", u=4, i=4),
+                    w3_bf[:, blk * 4 * P:(blk + 1) * 4 * P].rearrange("p (c u i) -> p c i u", u=4, i=4),
                     raw.rearrange("p i (c u) -> p c i u", u=4),
                 )
-            nc.vector.quantize_mx(w3_q[n][:].bitcast(FP8X4), w3_sc[n][:], rounded3[:])
+            nc.vector.quantize_mx(w3_q[n][:].bitcast(FP8X4), w3_sc[n][:], w3_bf[:])
 
         gather_words(0, 0, S)
         quantise_w1(0, 0)
@@ -166,40 +166,40 @@ def tile_list_drum_hit_matcher_kernel(
         w2_dealt = held([P, 2 * H], U8, "w2_dealt")
         w2_sc = held([P, H], U8, "w2_sc")
         nc.scalar.copy(
-            w2_dealt[:].bitcast(U16).rearrange("p (k t m) -> p k t m", k=2, t=4),
-            w2_raw[:].bitcast(U16).rearrange("p (k m t) -> p k t m", k=2, t=4),
+            w2_dealt[:].bitcast(U16).rearrange("p (blk t m) -> p blk t m", blk=2, t=4),
+            w2_raw[:].bitcast(U16).rearrange("p (blk m t) -> p blk t m", blk=2, t=4),
         )
         nc.vector.tensor_copy(
-            w2_sc[:].rearrange("p (k t m) -> p k t m", k=2, t=4),
-            w2_sc_raw[:].rearrange("p (k m t) -> p k t m", k=2, t=4),
+            w2_sc[:].rearrange("p (blk t m) -> p blk t m", blk=2, t=4),
+            w2_sc_raw[:].rearrange("p (blk m t) -> p blk t m", blk=2, t=4),
         )
         gather_words(1, 0, S)
         quantise_w1(0, 1)
         quantise_w1(1, 1)
-        gather_words(2, 0, CHUNK)
-        gather_words(2, CHUNK, CHUNK)
-        gather_words(2, HALF, HALF)
 
         spans = ((0, CHUNK), (CHUNK, CHUNK), (HALF, HALF))
+        for j0, width in spans:
+            gather_words(TAB2, j0, width)
+
         act = {(blk, j0): held([P, 4, width], F32, f"act{blk}_{j0}") for blk in range(2) for j0, width in spans}
 
-        def act_cols(blk, j0, width):
-            base = min(j0, HALF)
-            return act[blk, base][:, :, j0 - base:j0 - base + width]
+        def act_chunk(blk, c):
+            span = min(c * CHUNK, HALF)
+            return act[blk, span][:, :, c * CHUNK - span:(c + 1) * CHUNK - span]
 
         h_q = [held([P, S], U32, f"h_q{blk}") for blk in range(2)]
         h_sc = [held([P, S], U8, f"h_sc{blk}") for blk in range(2)]
 
-        def e_pass(sums, blk, t, j0, width, a, start, stop):
+        def e_pass(e_sum, blk, t, j0, width, a, start, stop):
             cols = slice(j0, j0 + width)
-            if a == 2:
+            if a == TAB2:
                 r0 = blk * PASS + t * P
                 lhs, lhs_sc = w2_dealt[:, 2 * r0:2 * (r0 + P)].bitcast(FP4X4), w2_sc[:, r0:r0 + P]
                 rhs_sc = v2_sc[:, cols]
             else:
                 lhs, lhs_sc = w1_q[a, blk][:, t * P:(t + 1) * P].bitcast(FP8X4), w1_sc[a, blk][:, t * P:(t + 1) * P]
                 rhs_sc = v_sc[4 * a:P, cols]
-            nc.tensor.matmul_mx(sums, lhs, lhs_sc, v[a][:, cols].bitcast(FP8X4), rhs_sc, start=start, stop=stop)
+            nc.tensor.matmul_mx(e_sum, lhs, lhs_sc, v[a][:, cols].bitcast(FP8X4), rhs_sc, start=start, stop=stop)
 
         def first_stage(blks, j0, width):
             per_bank = HALF // width
@@ -207,62 +207,58 @@ def tile_list_drum_hit_matcher_kernel(
                 (blk, u): e_psum.tile([P, HALF], F32, name="e_bank") for blk in blks for u in range(4 // per_bank)
             }
 
-            def sums(blk, t):
+            def e_sum(blk, t):
                 c0 = t % per_bank * width
                 return banks[blk, t // per_bank][:, c0:c0 + width]
 
             for blk in blks:
                 for a in range(2):
                     for t in range(4):
-                        e_pass(sums(blk, t), blk, t, j0, width, a, a == 0 and t % per_bank == 0, False)
+                        e_pass(e_sum(blk, t), blk, t, j0, width, a, a == 0 and t % per_bank == 0, False)
             for blk in blks:
                 for t in range(4):
-                    e_pass(sums(blk, t), blk, t, j0, width, 2, False, t % per_bank == per_bank - 1)
+                    e_pass(e_sum(blk, t), blk, t, j0, width, TAB2, False, t % per_bank == per_bank - 1)
                 for t in range(4):
-                    nc.scalar.activation(
-                        act[blk, j0][:, t, :], sums(blk, t), TANH, bias=bias_t[:, blk, t:t + 1]
-                    )
+                    nc.scalar.activation(act[blk, j0][:, t, :], e_sum(blk, t), TANH, bias=bias_t[:, blk, t:t + 1])
 
-        def apply_gain(blk, c):
-            j0, width = CHUNKS[c]
-            h_bf = held([P, 4 * width], BF16, f"h_bf{blk}{c}")
-            gains = gain_t[:, blk, :].rearrange("p (c t u) -> p c t u", c=1, u=1).to_broadcast([P, width // 4, 4, 4])
+        def gain_on_vector(blk, c):
+            h_bf = held([P, 4 * CHUNK], BF16, f"h_bf{blk}{c}")
+            gains = gain_t[:, blk, :].rearrange("p (x t u) -> p x t u", x=1, u=1).to_broadcast([P, CHUNK // 4, 4, 4])
             nc.vector.tensor_tensor(
-                h_bf[:].rearrange("p (c u t) -> p c t u", u=4, t=4),
-                act_cols(blk, j0, width).rearrange("p t (c u) -> p c t u", u=4),
+                h_bf[:].rearrange("p (x u t) -> p x t u", u=4, t=4),
+                act_chunk(blk, c).rearrange("p t (x u) -> p x t u", u=4),
                 gains, MULT,
             )
             return h_bf
 
-        def apply_gain_scalar(blk, c):
-            j0, width = CHUNKS[c]
-            planes = keep.tile([P, 4, width], BF16, name="h_planes", tag=f"planes{blk}{c}", align_bytes=64)
+        def gain_on_scalar(blk, c):
+            by_t = keep.tile([P, 4, CHUNK], BF16, name="h_planes", tag=f"planes{blk}{c}", align_bytes=64)
             for t in range(4):
-                nc.scalar.activation(planes[:, t, :], act_cols(blk, j0, width)[:, t, :], COPY, scale=gain_t[:, blk, t:t + 1])
-            h_bf = held([P, 4 * width], BF16, f"h_bf{blk}{c}")
+                nc.scalar.activation(by_t[:, t, :], act_chunk(blk, c)[:, t, :], COPY, scale=gain_t[:, blk, t:t + 1])
+            h_bf = held([P, 4 * CHUNK], BF16, f"h_bf{blk}{c}")
             nc.scalar.copy(
-                h_bf[:].rearrange("p (c u t) -> p c t u", u=4, t=4),
-                planes[:].rearrange("p t (c u) -> p c t u", u=4),
+                h_bf[:].rearrange("p (x u t) -> p x t u", u=4, t=4),
+                by_t[:].rearrange("p t (x u) -> p x t u", u=4),
             )
             return h_bf
 
         def quantise_h(blk, c, h_bf):
-            j0, width = CHUNKS[c]
-            nc.vector.quantize_mx(h_q[blk][:, j0:j0 + width].bitcast(FP8X4), h_sc[blk][:, j0:j0 + width], h_bf[:])
+            cols = slice(c * CHUNK, (c + 1) * CHUNK)
+            nc.vector.quantize_mx(h_q[blk][:, cols].bitcast(FP8X4), h_sc[blk][:, cols], h_bf[:])
 
-        def second_stage(n, j0, width, after=None):
+        def second_stage(n, j0, width, reuse=None):
             bank = y_psum.tile([P, HALF], F32, name="y_bank")
             cols = slice(j0, j0 + width)
             for blk in range(2):
-                rows = slice(blk * P, (blk + 1) * P)
+                w3_cols = slice(blk * P, (blk + 1) * P)
                 nc.tensor.matmul_mx(
-                    bank[:, 0:width], w3_q[n][:, rows].bitcast(FP8X4), w3_sc[n][:, rows],
+                    bank[:, 0:width], w3_q[n][:, w3_cols].bitcast(FP8X4), w3_sc[n][:, w3_cols],
                     h_q[blk][:, cols].bitcast(FP8X4), h_sc[blk][:, cols], start=(blk == 0), stop=(blk == 1),
                 )
-            if after is None:
+            if reuse is None:
                 y = yring.tile([P, HALF], F32, name="y")
             else:
-                y = keep.tile([P, HALF], F32, name="y_held", tag=after, align_bytes=64)
+                y = keep.tile([P, HALF], F32, name="y_held", tag=reuse, align_bytes=64)
             nc.scalar.copy(y[:, 0:width], bank[:, 0:width])
             nc.vector.tensor_tensor(
                 pages[n][:].indirect(list3[:, j0 // 16:(j0 + width) // 16]), y[:, 0:width], wgo_t[:, cols], MULT
@@ -273,7 +269,7 @@ def tile_list_drum_hit_matcher_kernel(
 
         first_stage((0, 1), 0, CHUNK)
         for blk in range(2):
-            quantise_h(blk, 0, apply_gain(blk, 0))
+            quantise_h(blk, 0, gain_on_vector(blk, 0))
         quantise_w3(0)
         second_stage(0, 0, CHUNK)
         first_stage((0,), CHUNK, CHUNK)
@@ -281,22 +277,24 @@ def tile_list_drum_hit_matcher_kernel(
         second_stage(1, 0, CHUNK)
         first_stage((1,), CHUNK, CHUNK)
         for blk in range(2):
-            quantise_h(blk, 1, apply_gain(blk, 1))
+            quantise_h(blk, 1, gain_on_vector(blk, 1))
         quantise_w3(2)
         second_stage(2, 0, CHUNK)
         for n in range(3):
             second_stage(n, CHUNK, CHUNK)
+
         first_stage((0,), HALF, HALF)
         first_stage((1,), HALF, HALF)
         quantise_w3(3)
-        quantise_h(0, 2, apply_gain(0, 2))
-        quantise_h(1, 2, apply_gain_scalar(1, 2))
-        second_stage(3, 0, HALF, after="planes12")
+        quantise_h(0, 2, gain_on_vector(0, 2))
+        quantise_h(1, 2, gain_on_scalar(1, 2))
+        second_stage(3, 0, HALF, reuse="planes12")
         second_stage(0, HALF, CHUNK)
         for blk in range(2):
-            quantise_h(blk, 3, apply_gain_scalar(blk, 3))
-        second_stage(1, HALF, CHUNK, after="planes13")
+            quantise_h(blk, 3, gain_on_scalar(blk, 3))
+        second_stage(1, HALF, CHUNK, reuse="planes13")
         second_stage(2, HALF, CHUNK)
+
         for n in range(3):
             second_stage(n, HALF + CHUNK, CHUNK)
             store(n)

from contextlib import ExitStack

import concourse.mybir as mybir

K, K2, H, N, T, S, T2 = 1024, 512, 1024, 512, 2048, 1024, 2048
FLOPS = 2 * S * (K * H + K2 * H + H * N)

F32 = mybir.dt.float32
BF16 = mybir.dt.bfloat16
I32 = mybir.dt.int32
U32 = mybir.dt.uint32
U16 = mybir.dt.uint16
U8 = mybir.dt.uint8
FP8X4 = mybir.dt.float8_e4m3fn_x4
FP4X4 = mybir.dt.float4_e2m1fn_x4
MULT = mybir.AluOpType.mult
TANH = mybir.ActivationFunctionType.Tanh
COPY = mybir.ActivationFunctionType.Copy

P = 128
PASS = 512
HALF = 512
CHUNK = 256
W3_COLS = 256
TAB2 = 2
Y_BUFS = 6
E_BANKS, Y_BANKS = 6, 2


def tile_list_drum_hit_matcher_kernel(
    tc, tab_words, tab_scales, offs, tab2_words, tab2_scales, offs2, offs3,
    w1, w2_words, w2_scales, b, gain, w3, page1, wgo, out,
):
    nc = tc.nc
    with ExitStack() as ctx:
        keep = ctx.enter_context(tc.tile_pool(name="keep", bufs=1))
        ring = ctx.enter_context(tc.tile_pool(name="ring", bufs=2))
        yring = ctx.enter_context(tc.tile_pool(name="yring", bufs=Y_BUFS))
        e_psum = ctx.enter_context(tc.psum_pool(name="e_psum", bufs=E_BANKS))
        y_psum = ctx.enter_context(tc.psum_pool(name="y_psum", bufs=Y_BANKS))

        def held(shape, dtype, name):
            return keep.tile(shape, dtype, name=name, align_bytes=64)

        lists = keep.tile([P, S // 16], U16, name="lists")
        list2 = keep.tile([P, S // 16], U16, name="list2")
        list3 = keep.tile([P, S // 16], U16, name="list3")

        tab_sc = keep.tile([P, T], U8, name="tab_sc", tag="scale_window", align_bytes=64)
        tab2_sc = held([P, T], U8, "tab2_sc")
        w2_sc_raw = held([P, H], U8, "w2_sc_raw")
        tab2_sc_in = held([P, T], U8, "tab2_sc_in")
        nc.gpsimd.memset(w2_sc_raw[:].bitcast(I32), 0)
        nc.vector.memset(tab_sc[:].bitcast(I32), 0)
        nc.vector.memset(tab2_sc[:].bitcast(I32), 0)

        tab_w = [held([P, T], I32, f"tab_w{a}") for a in range(3)]
        w1_raw = {(a, blk): held([P, 4, PASS], F32, f"w1_raw{a}{blk}") for blk in range(2) for a in range(2)}
        w3_raw = {(hf, blk): held([P, 4, W3_COLS], F32, f"w3_raw{hf}{blk}") for hf in range(2) for blk in range(2)}
        w2_raw = held([P, 2 * H], U8, "w2_raw")
        bias_t = held([P, 2, 4], F32, "bias_t")
        gain_t = held([P, 2, 4], F32, "gain_t")
        wgo_t = held([P, S], F32, "wgo_t")
        pages = [held([P, T2], F32, f"page{n}") for n in range(4)]

        def load_words(dst, words):
            nc.sync.dma_start(dst[:], words.rearrange("p t i -> p (t i)").bitcast(I32))

        def load_scale_rows(dst, scales):
            for d in range(4):
                nc.sync.dma_start(dst[32 * d:32 * d + 4, :].bitcast(I32), scales[4 * d:4 * d + 4, :].bitcast(I32))

        def load_w1(a, blk):
            rows = w1[a * PASS:(a + 1) * PASS, blk * PASS:(blk + 1) * PASS]
            nc.sync.dma_start(w1_raw[a, blk][:], rows.rearrange("(p i) c -> p i c", i=4))

        def load_w3(hf):
            for blk in range(2):
                rows = w3[blk * PASS:(blk + 1) * PASS, hf * W3_COLS:(hf + 1) * W3_COLS]
                nc.sync.dma_start(w3_raw[hf, blk][:], rows.rearrange("(p i) c -> p i c", i=4))

        def load_page(n):
            nc.sync.dma_start(pages[n][:], page1[n * P:(n + 1) * P, :])

        nc.sync.dma_start(lists[:], offs)
        load_words(tab_w[0], tab_words[0])
        nc.sync.dma_start(list2[:], offs2)
        load_scale_rows(tab2_sc_in, tab2_scales[0])
        load_w1(0, 0)
        for a in range(2):
            for s in range(2):
                nc.sync.dma_start(tab_sc[4 * a + s:P:16, :].bitcast(I32), tab_scales[a, s:16:2, :].bitcast(I32))
        load_w1(1, 0)
        nc.sync.dma_start(w2_raw[:].bitcast(I32), w2_words[0].bitcast(I32))
        load_words(tab_w[1], tab_words[1])
        load_w1(0, 1)
        load_scale_rows(w2_sc_raw, w2_scales[0])

        for d in range(4):
            quadrant = slice(32 * d, 32 * d + 4)
            nc.vector.tensor_copy(tab2_sc[quadrant, :].bitcast(I32), tab2_sc_in[quadrant, :].bitcast(I32))

        v_sc_got = held([P, S], U8, "v_sc_got")
        v_sc = held([P, S], U8, "v_sc")
        nc.vector.tensor_copy(v_sc_got[:], tab_sc[:].indirect(lists[:]))
        nc.vector.tensor_copy(v_sc[:].bitcast(I32), v_sc_got[:].bitcast(I32))

        def move_odd_rows(a):
            for s in range(2):
                nc.sync.dma_start(
                    v_sc[4 * a + 2 + s:P:32, :].bitcast(I32), v_sc_got[16 + 4 * a + s:P:32, :].bitcast(I32)
                )

        move_odd_rows(0)
        load_w1(1, 1)
        move_odd_rows(1)

        load_words(tab_w[TAB2], tab2_words[0])
        nc.sync.dma_start(bias_t[:], b.rearrange("(blk p t) -> p blk t", p=P, t=4))
        nc.sync.dma_start(gain_t[:], gain.rearrange("(blk p t) -> p blk t", p=P, t=4))
        load_w3(0)
        nc.sync.dma_start(list3[:], offs3)
        nc.sync.dma_start(wgo_t[:], wgo)
        load_page(0)
        load_page(1)
        load_w3(1)
        load_page(2)
        load_page(3)

        v = [held([P, S], U32, f"v{a}") for a in range(3)]

        def gather_words(a, j0, width):
            offsets = (list2 if a == TAB2 else lists)[:, j0 // 16:(j0 + width) // 16]
            nc.vector.tensor_copy(v[a][:, j0:j0 + width], tab_w[a][:].bitcast(U32).indirect(offsets))

        w1_q = {(a, blk): held([P, PASS], U32, f"w1_q{a}{blk}") for a, blk in w1_raw}
        w1_sc = {(a, blk): held([P, PASS], U8, f"w1_sc{a}{blk}") for a, blk in w1_raw}

        def quantise_w1(a, blk):
            w1_bf = ring.tile([P, 4 * PASS], BF16, name="w1_bf", align_bytes=64)
            nc.scalar.copy(
                w1_bf[:].rearrange("p (t m i) -> p m i t", t=4, i=4),
                w1_raw[a, blk][:].rearrange("p i (m t) -> p m i t", t=4),
            )
            nc.vector.quantize_mx(w1_q[a, blk][:].bitcast(FP8X4), w1_sc[a, blk][:], w1_bf[:])

        w3_q = [held([P, 2 * P], U32, f"w3_q{n}") for n in range(4)]
        w3_sc = [held([P, 2 * P], U8, f"w3_sc{n}") for n in range(4)]

        def quantise_w3(n):
            w3_bf = ring.tile([P, 2 * 4 * P], BF16, name="w3_bf", align_bytes=64)
            for blk in range(2):
                raw = w3_raw[n // 2, blk][:, :, n % 2 * P:(n % 2 + 1) * P]
                nc.scalar.copy(
                    w3_bf[:, blk * 4 * P:(blk + 1) * 4 * P].rearrange("p (c u i) -> p c i u", u=4, i=4),
                    raw.rearrange("p i (c u) -> p c i u", u=4),
                )
            nc.vector.quantize_mx(w3_q[n][:].bitcast(FP8X4), w3_sc[n][:], w3_bf[:])

        gather_words(0, 0, S)
        quantise_w1(0, 0)
        v2_sc = keep.tile([P, S], U8, name="v2_sc", tag="scale_window", align_bytes=64)
        nc.vector.tensor_copy(v2_sc[:], tab2_sc[:].indirect(list2[:]))
        quantise_w1(1, 0)

        w2_dealt = held([P, 2 * H], U8, "w2_dealt")
        w2_sc = held([P, H], U8, "w2_sc")
        nc.scalar.copy(
            w2_dealt[:].bitcast(U16).rearrange("p (blk t m) -> p blk t m", blk=2, t=4),
            w2_raw[:].bitcast(U16).rearrange("p (blk m t) -> p blk t m", blk=2, t=4),
        )
        nc.vector.tensor_copy(
            w2_sc[:].rearrange("p (blk t m) -> p blk t m", blk=2, t=4),
            w2_sc_raw[:].rearrange("p (blk m t) -> p blk t m", blk=2, t=4),
        )
        gather_words(1, 0, S)
        quantise_w1(0, 1)
        quantise_w1(1, 1)

        spans = ((0, CHUNK), (CHUNK, CHUNK), (HALF, HALF))
        for j0, width in spans:
            gather_words(TAB2, j0, width)

        act = {(blk, j0): held([P, 4, width], F32, f"act{blk}_{j0}") for blk in range(2) for j0, width in spans}

        def act_chunk(blk, c):
            span = min(c * CHUNK, HALF)
            return act[blk, span][:, :, c * CHUNK - span:(c + 1) * CHUNK - span]

        h_q = [held([P, S], U32, f"h_q{blk}") for blk in range(2)]
        h_sc = [held([P, S], U8, f"h_sc{blk}") for blk in range(2)]

        def e_pass(e_sum, blk, t, j0, width, a, start, stop):
            cols = slice(j0, j0 + width)
            if a == TAB2:
                r0 = blk * PASS + t * P
                lhs, lhs_sc = w2_dealt[:, 2 * r0:2 * (r0 + P)].bitcast(FP4X4), w2_sc[:, r0:r0 + P]
                rhs_sc = v2_sc[:, cols]
            else:
                lhs, lhs_sc = w1_q[a, blk][:, t * P:(t + 1) * P].bitcast(FP8X4), w1_sc[a, blk][:, t * P:(t + 1) * P]
                rhs_sc = v_sc[4 * a:P, cols]
            nc.tensor.matmul_mx(e_sum, lhs, lhs_sc, v[a][:, cols].bitcast(FP8X4), rhs_sc, start=start, stop=stop)

        def first_stage(blks, j0, width):
            per_bank = HALF // width
            banks = {
                (blk, u): e_psum.tile([P, HALF], F32, name="e_bank") for blk in blks for u in range(4 // per_bank)
            }

            def e_sum(blk, t):
                c0 = t % per_bank * width
                return banks[blk, t // per_bank][:, c0:c0 + width]

            for blk in blks:
                for a in range(2):
                    for t in range(4):
                        e_pass(e_sum(blk, t), blk, t, j0, width, a, a == 0 and t % per_bank == 0, False)
            for blk in blks:
                for t in range(4):
                    e_pass(e_sum(blk, t), blk, t, j0, width, TAB2, False, t % per_bank == per_bank - 1)
                for t in range(4):
                    nc.scalar.activation(act[blk, j0][:, t, :], e_sum(blk, t), TANH, bias=bias_t[:, blk, t:t + 1])

        def gain_on_vector(blk, c):
            h_bf = held([P, 4 * CHUNK], BF16, f"h_bf{blk}{c}")
            gains = gain_t[:, blk, :].rearrange("p (x t u) -> p x t u", x=1, u=1).to_broadcast([P, CHUNK // 4, 4, 4])
            nc.vector.tensor_tensor(
                h_bf[:].rearrange("p (x u t) -> p x t u", u=4, t=4),
                act_chunk(blk, c).rearrange("p t (x u) -> p x t u", u=4),
                gains, MULT,
            )
            return h_bf

        def gain_on_scalar(blk, c):
            by_t = keep.tile([P, 4, CHUNK], BF16, name="h_planes", tag=f"planes{blk}{c}", align_bytes=64)
            for t in range(4):
                nc.scalar.activation(by_t[:, t, :], act_chunk(blk, c)[:, t, :], COPY, scale=gain_t[:, blk, t:t + 1])
            h_bf = held([P, 4 * CHUNK], BF16, f"h_bf{blk}{c}")
            nc.scalar.copy(
                h_bf[:].rearrange("p (x u t) -> p x t u", u=4, t=4),
                by_t[:].rearrange("p t (x u) -> p x t u", u=4),
            )
            return h_bf

        def quantise_h(blk, c, h_bf):
            cols = slice(c * CHUNK, (c + 1) * CHUNK)
            nc.vector.quantize_mx(h_q[blk][:, cols].bitcast(FP8X4), h_sc[blk][:, cols], h_bf[:])

        def second_stage(n, j0, width, reuse=None):
            bank = y_psum.tile([P, HALF], F32, name="y_bank")
            cols = slice(j0, j0 + width)
            for blk in range(2):
                w3_cols = slice(blk * P, (blk + 1) * P)
                nc.tensor.matmul_mx(
                    bank[:, 0:width], w3_q[n][:, w3_cols].bitcast(FP8X4), w3_sc[n][:, w3_cols],
                    h_q[blk][:, cols].bitcast(FP8X4), h_sc[blk][:, cols], start=(blk == 0), stop=(blk == 1),
                )
            if reuse is None:
                y = yring.tile([P, HALF], F32, name="y")
            else:
                y = keep.tile([P, HALF], F32, name="y_held", tag=reuse, align_bytes=64)
            nc.scalar.copy(y[:, 0:width], bank[:, 0:width])
            nc.vector.tensor_tensor(
                pages[n][:].indirect(list3[:, j0 // 16:(j0 + width) // 16]), y[:, 0:width], wgo_t[:, cols], MULT
            )

        def store(n):
            nc.sync.dma_start(out[n * P:(n + 1) * P, :], pages[n][:])

        first_stage((0, 1), 0, CHUNK)
        for blk in range(2):
            quantise_h(blk, 0, gain_on_vector(blk, 0))
        quantise_w3(0)
        second_stage(0, 0, CHUNK)
        first_stage((0,), CHUNK, CHUNK)
        quantise_w3(1)
        second_stage(1, 0, CHUNK)
        first_stage((1,), CHUNK, CHUNK)
        for blk in range(2):
            quantise_h(blk, 1, gain_on_vector(blk, 1))
        quantise_w3(2)
        second_stage(2, 0, CHUNK)
        for n in range(3):
            second_stage(n, CHUNK, CHUNK)

        first_stage((0,), HALF, HALF)
        first_stage((1,), HALF, HALF)
        quantise_w3(3)
        quantise_h(0, 2, gain_on_vector(0, 2))
        quantise_h(1, 2, gain_on_scalar(1, 2))
        second_stage(3, 0, HALF, reuse="planes12")
        second_stage(0, HALF, CHUNK)
        for blk in range(2):
            quantise_h(blk, 3, gain_on_scalar(blk, 3))
        second_stage(1, HALF, CHUNK, reuse="planes13")
        second_stage(2, HALF, CHUNK)

        for n in range(3):
            second_stage(n, HALF + CHUNK, CHUNK)
            store(n)
        second_stage(3, HALF, HALF)
        store(3)
